import numpy as np
import ml_dtypes


def mxq(x, axis, fmt="e4m3"):
    dtype, down = {"e4m3": (ml_dtypes.float8_e4m3fn, 7), "e5m2": (ml_dtypes.float8_e5m2, 14)}[fmt]
    v = np.moveaxis(np.asarray(x, np.float32).astype(ml_dtypes.bfloat16).astype(np.float64), axis, -1)
    blocks = v.reshape(v.shape[:-1] + (-1, 32))
    amax = np.abs(blocks).max(-1, keepdims=True)
    byte = np.maximum(np.where(amax > 0, np.frexp(amax)[1] - 1 + 127, 0) - down, 1)
    scale = np.exp2(byte - 127.0)
    codes = (blocks / scale).astype(np.float32).astype(dtype).astype(np.float64)
    return np.moveaxis((codes * scale).reshape(v.shape), -1, axis)


WIDE = False


def mx_kscale(k):
    if not WIDE:
        return np.ones(k)
    levels = np.array([10, -10, 5, -5, 0])
    if k % 512:
        return np.exp2(np.random.permutation(np.resize(levels, k // 32))).repeat(32)
    a = np.empty((k // 512, 16))
    for p in range(k // 512):
        a[p, :8] = np.random.permutation(np.resize(levels, 8))
        for g in range(8):
            far = levels[np.abs(levels - a[p, g]) >= 10]
            a[p, g + 8] = far[np.random.randint(len(far))]
    return np.exp2(a.ravel()).repeat(32)


BF16 = ml_dtypes.bfloat16


def bf(x):
    return np.asarray(x, np.float32).astype(BF16)


def f64(x):
    return np.asarray(x).astype(np.float64)


E2M1 = np.array([0.0, 0.5, 1.0, 1.5, 2.0, 3.0, 4.0, 6.0, -0.0, -0.5, -1.0, -1.5, -2.0, -3.0, -4.0, -6.0])


def pack_weight(w, fmt):
    k, n = w.shape
    w = f64(bf(w)).reshape(k // 32, 32, n)
    amax = np.abs(w).max(1)
    if fmt == "e4m3":
        byte = np.frexp(amax)[1] - 1 + 127 - 7
    else:
        mant, ex = np.frexp(amax / 6.0)
        byte = np.where(mant > 0.5, ex, ex - 1) + 127
    byte = np.clip(np.where(amax > 0, byte, 1), 1, 254)
    scaled = (w * np.exp2(127.0 - byte)[:, None, :]).reshape(k, n).astype(np.float32)
    by_word = np.ascontiguousarray(scaled.reshape(k // 512, 128, 4, n).transpose(0, 1, 3, 2))
    if fmt == "e4m3":
        words = by_word.astype(ml_dtypes.float8_e4m3fn).view(np.uint8)
    else:
        c = by_word.astype(ml_dtypes.float4_e2m1fn).view(np.uint8) & 0xF
        words = c[..., 0::2] | (c[..., 1::2] << 4)
    return np.ascontiguousarray(words), np.ascontiguousarray(byte.astype(np.uint8).reshape(k // 512, 16, n))


def unpack_weight(words, scales, fmt):
    g, p, n, _ = words.shape
    if fmt == "e4m3":
        vals = np.ascontiguousarray(words).view(ml_dtypes.float8_e4m3fn).astype(np.float64)
    else:
        nib = np.empty((g, p, n, 4), np.uint8)
        nib[..., 0::2] = words & 0xF
        nib[..., 1::2] = words >> 4
        vals = E2M1[nib]
    vals = vals * np.repeat(np.exp2(scales.astype(np.float64) - 127.0), 8, axis=1)[..., None]
    return vals.transpose(0, 1, 3, 2).reshape(g * 512, n)
def pack4(w):
    words, scales = pack_weight(w, "e2m1")
    return words.reshape(words.shape[0], 128, -1), scales


def unpack4(words, scales):
    return unpack_weight(words.reshape(words.shape[0], 128, -1, 2), scales, "e2m1")


T1, T2, M, R, E = 512, 1536, 1024, 1024, 512


def draw0():
    s1, s2, u = mx_kscale(T1), mx_kscale(T2), mx_kscale(R)
    archive = np.random.standard_normal((T2, R)) * 0.11 / np.sqrt(T2) / s2[:, None]
    old_words, old_scales = pack4(archive)
    net = np.random.standard_normal((R, E)) / np.sqrt(R) / u[:, None]
    net_words, net_scales = pack4(net)
    return {"seeds_new": bf(np.random.standard_normal((T1, M)) * s1[:, None]),
            "regions_new": bf(np.random.standard_normal((T1, R)) * 0.09 / np.sqrt(T1) / s1[:, None]),
            "seeds_old": bf(np.random.standard_normal((T2, M)) * s2[:, None]),
            "old_words": old_words, "old_scales": old_scales,
            "precision": bf(3.0 * (1 + 0.1 * np.random.standard_normal(R)) * u),
            "net_words": net_words, "net_scales": net_scales}


def core(seeds_new, regions_new, seeds_old, old_words, old_scales, precision, net_words, net_scales):
    r_new = mxq(f64(seeds_new), 0, "e4m3").T @ mxq(f64(regions_new), 0, "e4m3")
    r_old = mxq(f64(seeds_old), 0, "e4m3").T @ unpack4(old_words, old_scales)
    r = r_new + r_old
    z = np.log((1.0 + r) / (1.0 - r)) * f64(precision)
    return mxq(z, 1, "e4m3") @ unpack4(net_words, net_scales)


def e4m3fn_bytes(y):
    return np.clip(np.asarray(y, np.float64), -448.0, 448.0).astype(np.float32).astype(ml_dtypes.float8_e4m3fn).view(np.uint8)


def e4m3fn_values(b):
    return np.asarray(b, np.uint8).view(ml_dtypes.float8_e4m3fn).astype(np.float64)


def setup_inputs():
    d = draw0()
    x0 = np.asarray(d['seeds_old']).astype(np.float64)
    s = (np.max(np.abs(x0), axis=(1,), keepdims=True) / 448.0).astype(np.float32)
    out = {}
    for k, v in d.items():
        if k == 'seeds_old':
            out['seeds_old_bytes'] = e4m3fn_bytes(x0 / s.astype(np.float64))
            out['seeds_old_scale'] = s
        else:
            out[k] = v
    return out


def reference(seeds_new, regions_new, seeds_old_bytes, seeds_old_scale, old_words, old_scales, precision, net_words, net_scales):
    return core(seeds_new, regions_new, e4m3fn_values(seeds_old_bytes) * seeds_old_scale.astype(np.float64), old_words, old_scales, precision, net_words, net_scales)

@@ -1,0 +1,285 @@
+from contextlib import ExitStack
+
+import concourse.mybir as mybir
+from concourse.masks import make_identity
+
+T1, T2, M, R, E = 512, 1536, 1024, 1024, 512
+FLOPS = 2 * M * R * (T1 + T2) + 2 * M * R * E
+
+F32 = mybir.dt.float32
+BF16 = mybir.dt.bfloat16
+U32 = mybir.dt.uint32
+I32 = mybir.dt.int32
+U8 = mybir.dt.uint8
+FP8 = mybir.dt.float8_e4m3fn
+FP8X4 = mybir.dt.float8_e4m3fn_x4
+FP4X4 = mybir.dt.float4_e2m1fn_x4
+ACT = mybir.ActivationFunctionType
+ALU = mybir.AluOpType
+
+P = 128
+OLD = 3
+PASSES = 4
+CHUNK = 256
+CHUNKS = M // CHUNK
+TILES = M // P
+
+
+def tile_pooled_fisher_connectivity_s3_kernel(
+    tc, seeds_new, regions_new, seeds_old_bytes, seeds_old_scale, old_words, old_scales, precision, net_words, net_scales, out
+):
+    nc = tc.nc
+    with ExitStack() as ctx:
+        keep = ctx.enter_context(tc.tile_pool(name="keep", bufs=1))
+        chunked = ctx.enter_context(tc.tile_pool(name="chunked", bufs=CHUNKS))
+        work = ctx.enter_context(tc.tile_pool(name="work", bufs=3))
+        psum_r = ctx.enter_context(tc.psum_pool(name="psum_r", bufs=4))
+        psum_t = ctx.enter_context(tc.psum_pool(name="psum_t", bufs=2))
+        psum_o = ctx.enter_context(tc.psum_pool(name="psum_o", bufs=2))
+        ctx.enter_context(tc.manual_schedule())
+
+        rn_raw = keep.tile([P, 4, R], BF16, align_bytes=64)
+        sn_raw = keep.tile([P, 4, M], BF16, align_bytes=64)
+        so_raw = keep.tile([P, OLD, 4 * M], U8, align_bytes=64)
+        so_scale = keep.tile([P, OLD, 4], F32)
+        prec = keep.tile([P, 2, 4], BF16)
+        rn_grouped = keep.tile([P, R, 4], BF16, align_bytes=64)
+        rn_codes = keep.tile([P, R], U32, align_bytes=64)
+        rn_scales = keep.tile([P, R], U8, align_bytes=64)
+        d_words = keep.tile([P, OLD, 2 * R], U8, align_bytes=64)
+        d_scales = keep.tile([P, OLD, R], U8, align_bytes=64)
+        p_words = keep.tile([P, 2, 2 * E], U8, align_bytes=64)
+        p_scales = keep.tile([P, 2, E], U8, align_bytes=64)
+        ident = keep.tile([P, P], F32)
+        warm = keep.tile([P, 1], F32)
+
+        wide, grouped, codes, scales = [], [], [], []
+        for c in range(CHUNKS):
+            wide_c = chunked.tile([P, OLD, 4, CHUNK], BF16, align_bytes=64)
+            grouped_c = chunked.tile([P, PASSES, CHUNK, 4], BF16, align_bytes=64)
+            codes_c = chunked.tile([P, PASSES, CHUNK], U32, align_bytes=64)
+            scales_c = chunked.tile([P, PASSES, CHUNK], U8, align_bytes=64)
+            wide.append(wide_c)
+            grouped.append(grouped_c)
+            codes.append(codes_c)
+            scales.append(scales_c)
+
+        nc.gpsimd.memset(d_scales[:].rearrange("p g n -> p (g n)").bitcast(I32), 0)
+        nc.gpsimd.memset(p_scales[:].rearrange("p g n -> p (g n)").bitcast(I32), 0)
+        nc.vector.memset(warm[:], 1.0)
+        make_identity(nc, ident[:])
+
+        rn_view = regions_new.rearrange("(p t) n -> p t n", t=4)
+        sn_view = seeds_new.rearrange("(p t) n -> p t n", t=4)
+        so_view = seeds_old_bytes.rearrange("(g p t) n -> g p (t n)", p=P, t=4)
+        nc.scalar.dma_start(out=so_scale[:], in_=seeds_old_scale.rearrange("(g p t) o -> p g (t o)", p=P, t=4))
+        nc.sync.dma_start(out=rn_raw[:, :, 0:512], in_=rn_view[:, :, 0:512])
+        nc.sync.dma_start(out=so_raw[:, 0, :], in_=so_view[0])
+        nc.sync.dma_start(out=rn_raw[:, :, 512:1024], in_=rn_view[:, :, 512:1024])
+        nc.sync.dma_start(out=so_raw[:, 1, :], in_=so_view[1])
+        nc.sync.dma_start(out=sn_raw[:, :, 0:512], in_=sn_view[:, :, 0:512])
+        nc.sync.dma_start(out=so_raw[:, 2, :], in_=so_view[2])
+        nc.sync.dma_start(out=d_words[:], in_=old_words.rearrange("g p w -> p g w"))
+        for q in range(4):
+            nc.sync.dma_start(
+                out=d_scales[32 * q : 32 * q + 4].rearrange("p g n -> p (g n)").bitcast(I32).rearrange("p (g n) -> p g n", g=OLD),
+                in_=old_scales[:, 4 * q : 4 * q + 4, :].bitcast(I32).rearrange("g r n -> r g n"),
+            )
+        nc.sync.dma_start(out=sn_raw[:, :, 512:1024], in_=sn_view[:, :, 512:1024])
+        nc.sync.dma_start(out=p_words[:], in_=net_words.rearrange("g p w -> p g w"))
+        for q in range(4):
+            nc.sync.dma_start(
+                out=p_scales[32 * q : 32 * q + 4].rearrange("p g n -> p (g n)").bitcast(I32).rearrange("p (g n) -> p g n", g=2),
+                in_=net_scales[:, 4 * q : 4 * q + 4, :].bitcast(I32).rearrange("g r n -> r g n"),
+            )
+        nc.sync.dma_start(out=prec[:], in_=precision.rearrange("(g p t) -> p g t", p=P, t=4))
+
+        nc.scalar.activation(out=warm[:], in_=warm[:], func=ACT.Ln)
+
+        def interleave(dst, src):
+            nc.vector.tensor_copy(
+                out=dst.rearrange("p (c i) t -> p c t i", i=4),
+                in_=src.rearrange("p t (c i) -> p c t i", i=4),
+            )
+
+        def irn(h):
+            interleave(rn_grouped[:, 512 * h : 512 * h + 512, :], rn_raw[:, :, 512 * h : 512 * h + 512])
+
+        def qrn(h):
+            cols = slice(512 * h, 512 * h + 512)
+            nc.vector.quantize_mx(
+                out=rn_codes[:, cols].bitcast(FP8X4), scales=rn_scales[:, cols], in_=rn_grouped[:, cols, :].rearrange("p n t -> p (n t)")
+            )
+
+        def widen(c, g):
+            for t in range(4):
+                lo = t * M + CHUNK * c
+                nc.scalar.activation(
+                    out=wide[c][:, g, t, :], in_=so_raw[:, g, lo : lo + CHUNK].bitcast(FP8), func=ACT.Copy, scale=so_scale[:, g, t : t + 1]
+                )
+
+        def il(c, k):
+            src = sn_raw[:, :, CHUNK * c : CHUNK * c + CHUNK] if k == 0 else wide[c][:, k - 1, :, :]
+            interleave(grouped[c][:, k, :, :], src)
+
+        def quant(c, k0, k1):
+            nc.vector.quantize_mx(
+                out=codes[c][:, k0:k1, :].rearrange("p k n -> p (k n)").bitcast(FP8X4),
+                scales=scales[c][:, k0:k1, :].rearrange("p k n -> p (k n)"),
+                in_=grouped[c][:, k0:k1, :, :].rearrange("p k n t -> p (k n t)"),
+            )
+
+        r_banks = {}
+
+        def corr(i):
+            c, j = divmod(i, 2)
+            cols = slice(P * j, P * j + P)
+            banks = []
+            for h in range(2):
+                r_bank = psum_r.tile([P, 512], F32)
+                banks.append(r_bank)
+            r_banks[i] = banks
+            for n, k in enumerate((1, 2, 0, 3)):
+                for h in range(2):
+                    lhsT = codes[c][:, k, cols].bitcast(FP8X4)
+                    if k == 0:
+                        rhs = rn_codes[:, 512 * h : 512 * h + 512].bitcast(FP8X4)
+                        rhs_scale = rn_scales[:, 512 * h : 512 * h + 512]
+                    else:
+                        rhs = d_words[:, k - 1, 1024 * h : 1024 * h + 1024].bitcast(FP4X4)
+                        rhs_scale = d_scales[:, k - 1, 512 * h : 512 * h + 512]
+                    nc.tensor.matmul_mx(
+                        out=banks[h][:], lhsT=lhsT, lhsT_scale=scales[c][:, k, cols], rhs=rhs, rhs_scale=rhs_scale, start=(n == 0), stop=(n == 3)
+                    )
+
+        logs = {}
+
+        def logarithms(i, h):
+            view = r_banks[i][h][:].rearrange("p (m t) -> p t m", t=4)
+            ln_plus = work.tile([P, 4, P], F32)
+            ln_minus = work.tile([P, 4, P], F32)
+            nc.scalar.activation(out=ln_plus[:], in_=view, func=ACT.Ln, bias=1.0, scale=1.0)
+            nc.scalar.activation(out=ln_minus[:], in_=view, func=ACT.Ln, bias=1.0, scale=-1.0)
+            logs[i, h] = (ln_plus, ln_minus)
+
+        fisher = {}
+
+        def sub(i, h):
+            diff = work.tile([P, 4, P], F32)
+            a, b = logs[i, h]
+            nc.vector.tensor_tensor(out=diff[:], in0=a[:], in1=b[:], op=ALU.subtract)
+            fisher[i, h] = diff
+
+        turned = {}
+
+        def turn(i, h):
+            turned_bank = psum_t.tile([P, 4, P], F32)
+            for t in range(4):
+                nc.tensor.transpose(turned_bank[:, t, :], fisher[i, h][:, t, :], ident[:])
+            turned[i, h] = turned_bank
+
+        z_grouped, z_codes = {}, {}
+
+        def z_tile(i):
+            z_g = work.tile([P, 2, P, 4], BF16, align_bytes=64)
+            z_grouped[i] = z_g
+
+        def weigh(i, h):
+            nc.vector.tensor_tensor(
+                out=z_grouped[i][:, h, :, :],
+                in0=turned[i, h][:].rearrange("p t n -> p n t"),
+                in1=prec[:, h, :].unsqueeze(1).to_broadcast([P, P, 4]),
+                op=ALU.mult,
+            )
+
+        def quant_z(i):
+            z_c = work.tile([P, 2, P], U32, align_bytes=64)
+            z_s = work.tile([P, 2, P], U8, align_bytes=64)
+            nc.vector.quantize_mx(
+                out=z_c[:].rearrange("p h n -> p (h n)").bitcast(FP8X4),
+                scales=z_s[:].rearrange("p h n -> p (h n)"),
+                in_=z_grouped[i][:].rearrange("p h n t -> p (h n t)"),
+            )
+            z_codes[i] = (z_c, z_s)
+
+        o_banks = {}
+
+        def project(i):
+            o_bank = psum_o.tile([P, E], F32)
+            z_c, z_s = z_codes[i]
+            for h in range(2):
+                nc.tensor.matmul_mx(
+                    out=o_bank[:], lhsT=z_c[:, h, :].bitcast(FP8X4), lhsT_scale=z_s[:, h, :],
+                    rhs=p_words[:, h, :].bitcast(FP4X4), rhs_scale=p_scales[:, h, :], start=(h == 0), stop=(h == 1),
+                )
+            o_banks[i] = o_bank
+
+        def store(i):
+            o_sb = work.tile([P, E], F32)
+            nc.scalar.copy(out=o_sb[:], in_=o_banks[i][:])
+            nc.sync.dma_start(out=out[P * i : P * i + P, :], in_=o_sb[:])
+
+        for c, g in ((0, 0), (1, 0), (0, 1), (1, 1), (0, 2), (1, 2), (2, 0)):
+            widen(c, g)
+        irn(0)
+        qrn(0)
+        irn(1)
+        il(0, 1)
+        qrn(1)
+        il(0, 2)
+        quant(0, 1, 2)
+        il(0, 0)
+        quant(0, 2, 3)
+        il(1, 1)
+        quant(0, 0, 1)
+        il(0, 3)
+        il(1, 0)
+        quant(0, 3, 4)
+        corr(0)
+
+        v_fill = {
+            (0, 0): [(il, 1, 2), (quant, 1, 0, 2), (il, 1, 3)],
+            (0, 1): [(quant, 1, 2, 4)],
+            (0, 2): [(il, 2, 1)],
+            (0, 3): [(il, 2, 2)],
+            (1, 1): [(il, 2, 3)],
+            (1, 2): [(il, 2, 0)],
+            (1, 3): [(quant, 2, 0, 2)],
+            (2, 1): [(quant, 2, 2, 4)],
+            (2, 2): [(il, 3, 1)],
+            (2, 3): [(il, 3, 2)],
+            (3, 1): [(il, 3, 3)],
+            (3, 2): [(il, 3, 0)],
+            (3, 3): [(quant, 3, 0, 2)],
+            (4, 2): [(quant, 3, 2, 4)],
+        }
+        s_fill = {0: [(2, 1), (2, 2)], 1: [(3, 0)], 2: [(3, 1)], 3: [(3, 2)]}
+
+        def fill(i, slot):
+            for entry in v_fill.get((i, slot), []):
+                entry[0](*entry[1:])
+
+        for i in range(TILES):
+            z_tile(i)
+            logarithms(i, 0)
+            logarithms(i, 1)
+            for c, g in s_fill.get(i, []):
+                widen(c, g)
+            fill(i, 0)
+            if i + 1 < TILES:
+                corr(i + 1)
+            if i > 0:
+                project(i - 1)
+                store(i - 1)
+            sub(i, 0)
+            fill(i, 1)
+            sub(i, 1)
+            turn(i, 0)
+            turn(i, 1)
+            fill(i, 2)
+            weigh(i, 0)
+            weigh(i, 1)
+            fill(i, 3)
+            quant_z(i)
+        project(TILES - 1)
+        store(TILES - 1)

@@ -18,268 +18,363 @@ ACT = mybir.ActivationFunctionType
 ALU = mybir.AluOpType
 
 P = 128
-OLD = 3
-PASSES = 4
+PACK = 4
+GROUPS = T2 // (P * PACK)
+PASSES = 1 + GROUPS
+HALF = 512
 CHUNK = 256
-CHUNKS = M // CHUNK
 TILES = M // P
+
+PASS_ORDER = (2, 1, 3, 0)
+
+WIDEN = {0: ((2, 2),), 1: ((2, 3), (3, 2)), 2: ((3, 3),)}
+SCALAR_INTERLEAVE = {2: ((3, 0),), 3: ((3, 2),)}
+BEFORE_DIFFERENCE = {1: ((2, 0),)}
+AFTER_TURN = {0: ((1, 3),), 1: ((3, 1), (2, 2)), 2: ((2, 3), (3, 3))}
+QUANTISE_CHUNK = {2: 2, 4: 3}
+
+PSUM_DIFFERENCE = (1, 2)
+WEIGH_LATE = (2, 4)
 
 
 def tile_pooled_fisher_connectivity_s3_kernel(
-    tc, seeds_new, regions_new, seeds_old_bytes, seeds_old_scale, old_words, old_scales, precision, net_words, net_scales, out
+    tc,
+    seeds_new,
+    regions_new,
+    seeds_old_bytes,
+    seeds_old_scale,
+    old_words,
+    old_scales,
+    precision,
+    net_words,
+    net_scales,
+    out,
 ):
     nc = tc.nc
     with ExitStack() as ctx:
         keep = ctx.enter_context(tc.tile_pool(name="keep", bufs=1))
-        chunked = ctx.enter_context(tc.tile_pool(name="chunked", bufs=CHUNKS))
-        work = ctx.enter_context(tc.tile_pool(name="work", bufs=3))
+        old_pool = ctx.enter_context(tc.tile_pool(name="old", bufs=2 * GROUPS))
+        chunk_pool = ctx.enter_context(tc.tile_pool(name="chunks", bufs=M // CHUNK))
+        work = ctx.enter_context(tc.tile_pool(name="work", bufs=4))
         psum_r = ctx.enter_context(tc.psum_pool(name="psum_r", bufs=4))
-        psum_t = ctx.enter_context(tc.psum_pool(name="psum_t", bufs=2))
-        psum_o = ctx.enter_context(tc.psum_pool(name="psum_o", bufs=2))
+        psum_turn = ctx.enter_context(tc.psum_pool(name="psum_turn", bufs=2))
+        psum_out = ctx.enter_context(tc.psum_pool(name="psum_out", bufs=2))
         ctx.enter_context(tc.manual_schedule())
 
-        rn_raw = keep.tile([P, 4, R], BF16, align_bytes=64)
-        sn_raw = keep.tile([P, 4, M], BF16, align_bytes=64)
-        so_raw = keep.tile([P, OLD, 4 * M], U8, align_bytes=64)
-        so_scale = keep.tile([P, OLD, 4], F32)
-        prec = keep.tile([P, 2, 4], BF16)
-        rn_grouped = keep.tile([P, R, 4], BF16, align_bytes=64)
-        rn_codes = keep.tile([P, R], U32, align_bytes=64)
-        rn_scales = keep.tile([P, R], U8, align_bytes=64)
-        d_words = keep.tile([P, OLD, 2 * R], U8, align_bytes=64)
-        d_scales = keep.tile([P, OLD, R], U8, align_bytes=64)
+        regions_a = keep.tile([P, PACK, 256], BF16, align_bytes=64)
+        regions_b = keep.tile([P, PACK, 256], BF16, align_bytes=64)
+        regions_c = keep.tile([P, PACK, HALF], BF16, align_bytes=64)
+        region_loads = ((regions_a, 0), (regions_b, 256), (regions_c, HALF))
+        new_a = keep.tile([P, PACK, HALF], BF16, align_bytes=64)
+        new_b = keep.tile([P, PACK, HALF], BF16, align_bytes=64)
+        new_raw = (new_a, new_b)
+        old_bytes = {}
+        for g in range(GROUPS):
+            for half in range(2):
+                old_bytes_tile = old_pool.tile([P, PACK, HALF], U8, align_bytes=64)
+                old_bytes[g, half] = old_bytes_tile
+        old_factor = keep.tile([P, GROUPS, PACK], F32)
+        d_words_a = keep.tile([P, GROUPS, 2 * HALF], U8, align_bytes=64)
+        d_words_b = keep.tile([P, GROUPS, 2 * HALF], U8, align_bytes=64)
+        d_words = (d_words_a, d_words_b)
+        d_scales = keep.tile([P, GROUPS, R], U8, align_bytes=64)
         p_words = keep.tile([P, 2, 2 * E], U8, align_bytes=64)
         p_scales = keep.tile([P, 2, E], U8, align_bytes=64)
-        ident = keep.tile([P, P], F32)
-        warm = keep.tile([P, 1], F32)
+        weights = keep.tile([P, 2, PACK], BF16)
 
+        regions_grouped = keep.tile([P, R, PACK], BF16, align_bytes=64)
+        regions_codes = keep.tile([P, R], U32, align_bytes=64)
+        regions_scales = keep.tile([P, R], U8, align_bytes=64)
         wide, grouped, codes, scales = [], [], [], []
-        for c in range(CHUNKS):
-            wide_c = chunked.tile([P, OLD, 4, CHUNK], BF16, align_bytes=64)
-            grouped_c = chunked.tile([P, PASSES, CHUNK, 4], BF16, align_bytes=64)
-            codes_c = chunked.tile([P, PASSES, CHUNK], U32, align_bytes=64)
-            scales_c = chunked.tile([P, PASSES, CHUNK], U8, align_bytes=64)
-            wide.append(wide_c)
-            grouped.append(grouped_c)
-            codes.append(codes_c)
-            scales.append(scales_c)
+        for c in range(M // CHUNK):
+            wide_tile = chunk_pool.tile([P, GROUPS, PACK, CHUNK], BF16, align_bytes=64)
+            grouped_tile = chunk_pool.tile([P, PASSES, CHUNK, PACK], BF16, align_bytes=64)
+            codes_tile = chunk_pool.tile([P, PASSES, CHUNK], U32, align_bytes=64)
+            scales_tile = chunk_pool.tile([P, PASSES, CHUNK], U8, align_bytes=64)
+            wide.append(wide_tile)
+            grouped.append(grouped_tile)
+            codes.append(codes_tile)
+            scales.append(scales_tile)
+
+        identity = keep.tile([P, P], F32)
+        one = keep.tile([P, 1], F32)
 
         nc.gpsimd.memset(d_scales[:].rearrange("p g n -> p (g n)").bitcast(I32), 0)
         nc.gpsimd.memset(p_scales[:].rearrange("p g n -> p (g n)").bitcast(I32), 0)
-        nc.vector.memset(warm[:], 1.0)
-        make_identity(nc, ident[:])
+        nc.vector.memset(one[:], 1.0)
+        make_identity(nc, identity[:])
 
-        rn_view = regions_new.rearrange("(p t) n -> p t n", t=4)
-        sn_view = seeds_new.rearrange("(p t) n -> p t n", t=4)
-        so_view = seeds_old_bytes.rearrange("(g p t) n -> g p (t n)", p=P, t=4)
-        nc.scalar.dma_start(out=so_scale[:], in_=seeds_old_scale.rearrange("(g p t) o -> p g (t o)", p=P, t=4))
-        nc.sync.dma_start(out=rn_raw[:, :, 0:512], in_=rn_view[:, :, 0:512])
-        nc.sync.dma_start(out=so_raw[:, 0, :], in_=so_view[0])
-        nc.sync.dma_start(out=rn_raw[:, :, 512:1024], in_=rn_view[:, :, 512:1024])
-        nc.sync.dma_start(out=so_raw[:, 1, :], in_=so_view[1])
-        nc.sync.dma_start(out=sn_raw[:, :, 0:512], in_=sn_view[:, :, 0:512])
-        nc.sync.dma_start(out=so_raw[:, 2, :], in_=so_view[2])
-        nc.sync.dma_start(out=d_words[:], in_=old_words.rearrange("g p w -> p g w"))
-        for q in range(4):
+        def load_regions(j):
+            tile, lo = region_loads[j]
             nc.sync.dma_start(
-                out=d_scales[32 * q : 32 * q + 4].rearrange("p g n -> p (g n)").bitcast(I32).rearrange("p (g n) -> p g n", g=OLD),
-                in_=old_scales[:, 4 * q : 4 * q + 4, :].bitcast(I32).rearrange("g r n -> r g n"),
+                out=tile[:], in_=regions_new.rearrange("(p t) n -> p t n", t=PACK)[:, :, lo : lo + tile[:].shape[2]]
             )
-        nc.sync.dma_start(out=sn_raw[:, :, 512:1024], in_=sn_view[:, :, 512:1024])
-        nc.sync.dma_start(out=p_words[:], in_=net_words.rearrange("g p w -> p g w"))
-        for q in range(4):
+
+        def load_new(half):
             nc.sync.dma_start(
-                out=p_scales[32 * q : 32 * q + 4].rearrange("p g n -> p (g n)").bitcast(I32).rearrange("p (g n) -> p g n", g=2),
-                in_=net_scales[:, 4 * q : 4 * q + 4, :].bitcast(I32).rearrange("g r n -> r g n"),
-            )
-        nc.sync.dma_start(out=prec[:], in_=precision.rearrange("(g p t) -> p g t", p=P, t=4))
-
-        nc.scalar.activation(out=warm[:], in_=warm[:], func=ACT.Ln)
-
-        def interleave(dst, src):
-            nc.vector.tensor_copy(
-                out=dst.rearrange("p (c i) t -> p c t i", i=4),
-                in_=src.rearrange("p t (c i) -> p c t i", i=4),
+                out=new_raw[half][:],
+                in_=seeds_new.rearrange("(p t) n -> p t n", t=PACK)[:, :, HALF * half : HALF * half + HALF],
             )
 
-        def irn(h):
-            interleave(rn_grouped[:, 512 * h : 512 * h + 512, :], rn_raw[:, :, 512 * h : 512 * h + 512])
+        def load_old(g, half):
+            rows = seeds_old_bytes.rearrange("(g p t) n -> g p t n", p=P, t=PACK)[g]
+            nc.sync.dma_start(out=old_bytes[g, half][:], in_=rows[:, :, HALF * half : HALF * half + HALF])
 
-        def qrn(h):
-            cols = slice(512 * h, 512 * h + 512)
-            nc.vector.quantize_mx(
-                out=rn_codes[:, cols].bitcast(FP8X4), scales=rn_scales[:, cols], in_=rn_grouped[:, cols, :].rearrange("p n t -> p (n t)")
-            )
+        def load_d(half):
+            words = old_words.rearrange("g p w -> p g w")
+            nc.sync.dma_start(out=d_words[half][:], in_=words[:, :, 2 * HALF * half : 2 * HALF * half + 2 * HALF])
 
-        def widen(c, g):
-            for t in range(4):
-                lo = t * M + CHUNK * c
-                nc.scalar.activation(
-                    out=wide[c][:, g, t, :], in_=so_raw[:, g, lo : lo + CHUNK].bitcast(FP8), func=ACT.Copy, scale=so_scale[:, g, t : t + 1]
+        def load_scale_rows(tile, rows, groups):
+            for q in range(4):
+                quadrant = tile[32 * q : 32 * q + 4].rearrange("p g n -> p (g n)").bitcast(I32)
+                nc.sync.dma_start(
+                    out=quadrant.rearrange("p (g n) -> p g n", g=groups),
+                    in_=rows[:, 4 * q : 4 * q + 4, :].bitcast(I32).rearrange("g r n -> r g n"),
                 )
 
-        def il(c, k):
-            src = sn_raw[:, :, CHUNK * c : CHUNK * c + CHUNK] if k == 0 else wide[c][:, k - 1, :, :]
-            interleave(grouped[c][:, k, :, :], src)
+        nc.scalar.dma_start(
+            out=old_factor[:], in_=seeds_old_scale.rearrange("(g p t) o -> p g (t o)", p=P, t=PACK)
+        )
+        load_old(0, 0)
+        load_regions(0)
+        load_regions(1)
+        load_scale_rows(d_scales, old_scales, GROUPS)
+        load_old(1, 0)
+        load_old(2, 0)
+        load_new(0)
+        load_d(0)
+        load_d(1)
+        load_regions(2)
+        for g in range(GROUPS):
+            load_old(g, 1)
+        load_new(1)
+        nc.sync.dma_start(out=p_words[:], in_=net_words.rearrange("g p w -> p g w"))
+        load_scale_rows(p_scales, net_scales, 2)
+        nc.sync.dma_start(out=weights[:], in_=precision.rearrange("(h p t) -> p h t", p=P, t=PACK))
 
-        def quant(c, k0, k1):
-            nc.vector.quantize_mx(
-                out=codes[c][:, k0:k1, :].rearrange("p k n -> p (k n)").bitcast(FP8X4),
-                scales=scales[c][:, k0:k1, :].rearrange("p k n -> p (k n)"),
-                in_=grouped[c][:, k0:k1, :, :].rearrange("p k n t -> p (k n t)"),
+        nc.scalar.activation(out=one[:], in_=one[:], func=ACT.Ln)
+
+        def widen(c, k):
+            cols = slice(CHUNK * (c % 2), CHUNK * (c % 2) + CHUNK)
+            for t in range(PACK):
+                nc.scalar.activation(
+                    out=wide[c][:, k - 1, t, :],
+                    in_=old_bytes[k - 1, c // 2][:, t, cols].bitcast(FP8),
+                    func=ACT.Copy,
+                    scale=old_factor[:, k - 1, t : t + 1],
+                )
+
+        def interleave(copy, dst, src):
+            copy(
+                out=dst.rearrange("p (n i) t -> p n t i", i=4),
+                in_=src.rearrange("p t (n i) -> p n t i", i=4),
             )
 
-        r_banks = {}
+        def interleave_regions(j):
+            tile, lo = region_loads[j]
+            interleave(nc.vector.tensor_copy, regions_grouped[:, lo : lo + tile[:].shape[2], :], tile[:])
 
-        def corr(i):
-            c, j = divmod(i, 2)
-            cols = slice(P * j, P * j + P)
-            banks = []
+        def quantise_regions(h):
+            cols = slice(HALF * h, HALF * h + HALF)
+            nc.vector.quantize_mx(
+                out=regions_codes[:, cols].bitcast(FP8X4),
+                scales=regions_scales[:, cols],
+                in_=regions_grouped[:, cols, :].rearrange("p n t -> p (n t)"),
+            )
+
+        def interleave_seeds(c, k, copy=nc.vector.tensor_copy):
+            if k == 0:
+                src = new_raw[c // 2][:, :, CHUNK * (c % 2) : CHUNK * (c % 2) + CHUNK]
+            else:
+                src = wide[c][:, k - 1, :, :]
+            interleave(copy, grouped[c][:, k, :, :], src)
+
+        def quantise_seeds(c, first, last):
+            nc.vector.quantize_mx(
+                out=codes[c][:, first:last, :].rearrange("p k n -> p (k n)").bitcast(FP8X4),
+                scales=scales[c][:, first:last, :].rearrange("p k n -> p (k n)"),
+                in_=grouped[c][:, first:last, :, :].rearrange("p k n t -> p (k n t)"),
+            )
+
+        r = {}
+
+        def take_banks(i):
             for h in range(2):
-                r_bank = psum_r.tile([P, 512], F32)
-                banks.append(r_bank)
-            r_banks[i] = banks
-            for n, k in enumerate((1, 2, 0, 3)):
-                for h in range(2):
-                    lhsT = codes[c][:, k, cols].bitcast(FP8X4)
-                    if k == 0:
-                        rhs = rn_codes[:, 512 * h : 512 * h + 512].bitcast(FP8X4)
-                        rhs_scale = rn_scales[:, 512 * h : 512 * h + 512]
-                    else:
-                        rhs = d_words[:, k - 1, 1024 * h : 1024 * h + 1024].bitcast(FP4X4)
-                        rhs_scale = d_scales[:, k - 1, 512 * h : 512 * h + 512]
+                r_bank = psum_r.tile([P, HALF], F32)
+                r[i, h] = r_bank
+
+        def correlate(tiles, h):
+            for n, k in enumerate(PASS_ORDER):
+                if k == 0:
+                    moving = regions_codes[:, HALF * h : HALF * h + HALF].bitcast(FP8X4)
+                    moving_scale = regions_scales[:, HALF * h : HALF * h + HALF]
+                else:
+                    moving = d_words[h][:, k - 1, :].bitcast(FP4X4)
+                    moving_scale = d_scales[:, k - 1, HALF * h : HALF * h + HALF]
+                for i in tiles:
+                    c, j = divmod(i, CHUNK // P)
+                    cols = slice(P * j, P * j + P)
                     nc.tensor.matmul_mx(
-                        out=banks[h][:], lhsT=lhsT, lhsT_scale=scales[c][:, k, cols], rhs=rhs, rhs_scale=rhs_scale, start=(n == 0), stop=(n == 3)
+                        out=r[i, h][:],
+                        lhsT=codes[c][:, k, cols].bitcast(FP8X4),
+                        lhsT_scale=scales[c][:, k, cols],
+                        rhs=moving,
+                        rhs_scale=moving_scale,
+                        start=(n == 0),
+                        stop=(n == PASSES - 1),
                     )
 
-        logs = {}
+        ln_plus, ln_minus, difference = {}, {}, {}
 
-        def logarithms(i, h):
-            view = r_banks[i][h][:].rearrange("p (m t) -> p t m", t=4)
-            ln_plus = work.tile([P, 4, P], F32)
-            ln_minus = work.tile([P, 4, P], F32)
-            nc.scalar.activation(out=ln_plus[:], in_=view, func=ACT.Ln, bias=1.0, scale=1.0)
-            nc.scalar.activation(out=ln_minus[:], in_=view, func=ACT.Ln, bias=1.0, scale=-1.0)
-            logs[i, h] = (ln_plus, ln_minus)
+        def take_logarithms(i, h):
+            if h == 0:
+                ln_plus_tile = work.tile([P, 2, PACK, P], F32)
+                ln_minus_tile = work.tile([P, 2, PACK, P], F32)
+                ln_plus[i], ln_minus[i] = ln_plus_tile, ln_minus_tile
+            by_t = r[i, h][:].rearrange("s (p t) -> s t p", t=PACK)
+            nc.scalar.activation(out=ln_plus[i][:, h], in_=by_t, func=ACT.Ln, bias=1.0, scale=1.0)
+            nc.scalar.activation(out=ln_minus[i][:, h], in_=by_t, func=ACT.Ln, bias=1.0, scale=-1.0)
 
-        fisher = {}
-
-        def sub(i, h):
-            diff = work.tile([P, 4, P], F32)
-            a, b = logs[i, h]
-            nc.vector.tensor_tensor(out=diff[:], in0=a[:], in1=b[:], op=ALU.subtract)
-            fisher[i, h] = diff
+        def form_difference(i, h):
+            if h == 0:
+                difference_tile = work.tile([P, 2, PACK, P], F32)
+                difference[i] = difference_tile
+            if i in PSUM_DIFFERENCE:
+                nc.vector.tensor_scalar(
+                    out=difference[i][:, h], in0=ln_minus[i][:, h], scalar1=-1.0, scalar2=None, op0=ALU.mult
+                )
+            else:
+                nc.vector.tensor_tensor(
+                    out=difference[i][:, h], in0=ln_plus[i][:, h], in1=ln_minus[i][:, h], op=ALU.subtract
+                )
 
         turned = {}
 
         def turn(i, h):
-            turned_bank = psum_t.tile([P, 4, P], F32)
-            for t in range(4):
-                nc.tensor.transpose(turned_bank[:, t, :], fisher[i, h][:, t, :], ident[:])
+            turned_bank = psum_turn.tile([P, PACK, P], F32)
             turned[i, h] = turned_bank
+            parts = (ln_plus[i], difference[i]) if i in PSUM_DIFFERENCE else (difference[i],)
+            for t in range(PACK):
+                for n, part in enumerate(parts):
+                    nc.tensor.matmul(
+                        turned_bank[:, t, :],
+                        lhsT=part[:, h, t, :],
+                        rhs=identity[:],
+                        start=(n == 0),
+                        stop=(n == len(parts) - 1),
+                        is_transpose=True,
+                    )
 
-        z_grouped, z_codes = {}, {}
+        z_codes, z_scales = {}, {}
 
-        def z_tile(i):
-            z_g = work.tile([P, 2, P, 4], BF16, align_bytes=64)
-            z_grouped[i] = z_g
+        def weigh_and_quantise(i):
+            z_grouped = work.tile([P, 2, P, PACK], BF16, align_bytes=64)
+            z_codes_tile = work.tile([P, 2, P], U32, align_bytes=64)
+            z_scales_tile = work.tile([P, 2, P], U8, align_bytes=64)
+            z_codes[i], z_scales[i] = z_codes_tile, z_scales_tile
+            for h in range(2):
+                nc.vector.tensor_tensor(
+                    out=z_grouped[:, h, :, :],
+                    in0=turned[i, h][:].rearrange("p t n -> p n t"),
+                    in1=weights[:, h, :].unsqueeze(1).to_broadcast([P, P, PACK]),
+                    op=ALU.mult,
+                )
+            for h in range(2):
+                nc.vector.quantize_mx(
+                    out=z_codes_tile[:, h, :].bitcast(FP8X4),
+                    scales=z_scales_tile[:, h, :],
+                    in_=z_grouped[:, h, :, :].rearrange("p n t -> p (n t)"),
+                )
 
-        def weigh(i, h):
-            nc.vector.tensor_tensor(
-                out=z_grouped[i][:, h, :, :],
-                in0=turned[i, h][:].rearrange("p t n -> p n t"),
-                in1=prec[:, h, :].unsqueeze(1).to_broadcast([P, P, 4]),
-                op=ALU.mult,
-            )
-
-        def quant_z(i):
-            z_c = work.tile([P, 2, P], U32, align_bytes=64)
-            z_s = work.tile([P, 2, P], U8, align_bytes=64)
-            nc.vector.quantize_mx(
-                out=z_c[:].rearrange("p h n -> p (h n)").bitcast(FP8X4),
-                scales=z_s[:].rearrange("p h n -> p (h n)"),
-                in_=z_grouped[i][:].rearrange("p h n t -> p (h n t)"),
-            )
-            z_codes[i] = (z_c, z_s)
-
-        o_banks = {}
+        out_bank = {}
 
         def project(i):
-            o_bank = psum_o.tile([P, E], F32)
-            z_c, z_s = z_codes[i]
+            out_bank_tile = psum_out.tile([P, E], F32)
+            out_bank[i] = out_bank_tile
             for h in range(2):
                 nc.tensor.matmul_mx(
-                    out=o_bank[:], lhsT=z_c[:, h, :].bitcast(FP8X4), lhsT_scale=z_s[:, h, :],
-                    rhs=p_words[:, h, :].bitcast(FP4X4), rhs_scale=p_scales[:, h, :], start=(h == 0), stop=(h == 1),
+                    out=out_bank_tile[:],
+                    lhsT=z_codes[i][:, h, :].bitcast(FP8X4),
+                    lhsT_scale=z_scales[i][:, h, :],
+                    rhs=p_words[:, h, :].bitcast(FP4X4),
+                    rhs_scale=p_scales[:, h, :],
+                    start=(h == 0),
+                    stop=(h == 1),
                 )
-            o_banks[i] = o_bank
 
         def store(i):
-            o_sb = work.tile([P, E], F32)
-            nc.scalar.copy(out=o_sb[:], in_=o_banks[i][:])
-            nc.sync.dma_start(out=out[P * i : P * i + P, :], in_=o_sb[:])
+            result = work.tile([P, E], F32)
+            nc.scalar.copy(out=result[:], in_=out_bank[i][:])
+            nc.sync.dma_start(out=out[P * i : P * i + P, :], in_=result[:])
 
-        for c, g in ((0, 0), (1, 0), (0, 1), (1, 1), (0, 2), (1, 2), (2, 0)):
-            widen(c, g)
-        irn(0)
-        qrn(0)
-        irn(1)
-        il(0, 1)
-        qrn(1)
-        il(0, 2)
-        quant(0, 1, 2)
-        il(0, 0)
-        quant(0, 2, 3)
-        il(1, 1)
-        quant(0, 0, 1)
-        il(0, 3)
-        il(1, 0)
-        quant(0, 3, 4)
-        corr(0)
+        def store_in_halves(i):
+            result_a = work.tile([P, E // 2], F32)
+            result_b = work.tile([P, E // 2], F32)
+            nc.scalar.copy(out=result_a[:], in_=out_bank[i][:, : E // 2])
+            nc.vector.tensor_copy(out=result_b[:], in_=out_bank[i][:, E // 2 :])
+            nc.sync.dma_start(out=out[P * i : P * i + P, : E // 2], in_=result_a[:])
+            nc.sync.dma_start(out=out[P * i : P * i + P, E // 2 :], in_=result_b[:])
 
-        v_fill = {
-            (0, 0): [(il, 1, 2), (quant, 1, 0, 2), (il, 1, 3)],
-            (0, 1): [(quant, 1, 2, 4)],
-            (0, 2): [(il, 2, 1)],
-            (0, 3): [(il, 2, 2)],
-            (1, 1): [(il, 2, 3)],
-            (1, 2): [(il, 2, 0)],
-            (1, 3): [(quant, 2, 0, 2)],
-            (2, 1): [(quant, 2, 2, 4)],
-            (2, 2): [(il, 3, 1)],
-            (2, 3): [(il, 3, 2)],
-            (3, 1): [(il, 3, 3)],
-            (3, 2): [(il, 3, 0)],
-            (3, 3): [(quant, 3, 0, 2)],
-            (4, 2): [(quant, 3, 2, 4)],
-        }
-        s_fill = {0: [(2, 1), (2, 2)], 1: [(3, 0)], 2: [(3, 1)], 3: [(3, 2)]}
-
-        def fill(i, slot):
-            for entry in v_fill.get((i, slot), []):
-                entry[0](*entry[1:])
+        for k in range(1, PASSES):
+            widen(0, k)
+            widen(1, k)
+        widen(2, 1)
+        widen(3, 1)
+        interleave_regions(0)
+        interleave_regions(1)
+        quantise_regions(0)
+        interleave_seeds(0, 1)
+        interleave_seeds(0, 2)
+        quantise_seeds(0, 1, 2)
+        interleave_seeds(0, 0)
+        quantise_seeds(0, 2, 3)
+        interleave_seeds(1, 0)
+        interleave_seeds(0, 3)
+        quantise_seeds(0, 0, 1)
+        quantise_seeds(0, 3, 4)
+        interleave_regions(2)
+        quantise_regions(1)
+        take_banks(0)
+        take_banks(1)
+        correlate((0, 1), 0)
+        correlate((0, 1), 1)
 
         for i in range(TILES):
-            z_tile(i)
-            logarithms(i, 0)
-            logarithms(i, 1)
-            for c, g in s_fill.get(i, []):
-                widen(c, g)
-            fill(i, 0)
-            if i + 1 < TILES:
-                corr(i + 1)
-            if i > 0:
-                project(i - 1)
-                store(i - 1)
-            sub(i, 0)
-            fill(i, 1)
-            sub(i, 1)
+            take_logarithms(i, 0)
+            for c, k in WIDEN.get(i, ()):
+                widen(c, k)
+            take_logarithms(i, 1)
+            if i > 1:
+                store(i - 2)
+            for c, k in SCALAR_INTERLEAVE.get(i, ()):
+                interleave_seeds(c, k, nc.scalar.copy)
+            if i == 0:
+                interleave_seeds(1, 1)
+                quantise_seeds(1, 0, 2)
+                interleave_seeds(1, 2)
+            for c, k in BEFORE_DIFFERENCE.get(i, ()):
+                interleave_seeds(c, k)
+            form_difference(i, 0)
+            form_difference(i, 1)
+            if i - 1 in WEIGH_LATE:
+                weigh_and_quantise(i - 1)
             turn(i, 0)
             turn(i, 1)
-            fill(i, 2)
-            weigh(i, 0)
-            weigh(i, 1)
-            fill(i, 3)
-            quant_z(i)
+            for c, k in AFTER_TURN.get(i, ()):
+                interleave_seeds(c, k)
+            if i == 0:
+                quantise_seeds(1, 2, 4)
+                interleave_seeds(2, 1)
+            if i in QUANTISE_CHUNK:
+                quantise_seeds(QUANTISE_CHUNK[i], 0, PASSES)
+            if i not in WEIGH_LATE:
+                weigh_and_quantise(i)
+            if i > 0:
+                project(i - 1)
+            if i + 2 < TILES:
+                take_banks(i + 2)
+                correlate((i + 2,), 0)
+                correlate((i + 2,), 1)
+        store(TILES - 2)
         project(TILES - 1)
-        store(TILES - 1)
+        store_in_halves(TILES - 1)

@@ -165,10 +165,7 @@ def tile_pooled_fisher_connectivity_s3_kernel(
                 )
 
         def interleave(copy, dst, src):
-            copy(
-                out=dst.rearrange("p (n i) t -> p n t i", i=4),
-                in_=src.rearrange("p t (n i) -> p n t i", i=4),
-            )
+            copy(out=dst, in_=src.rearrange("p t n -> p n t"))
 
         def interleave_regions(j):
             tile, lo = region_loads[j]

from contextlib import ExitStack

import concourse.mybir as mybir
from concourse.masks import make_identity

T1, T2, M, R, E = 512, 1536, 1024, 1024, 512
FLOPS = 2 * M * R * (T1 + T2) + 2 * M * R * E

F32 = mybir.dt.float32
BF16 = mybir.dt.bfloat16
U32 = mybir.dt.uint32
I32 = mybir.dt.int32
U8 = mybir.dt.uint8
FP8 = mybir.dt.float8_e4m3fn
FP8X4 = mybir.dt.float8_e4m3fn_x4
FP4X4 = mybir.dt.float4_e2m1fn_x4
ACT = mybir.ActivationFunctionType
ALU = mybir.AluOpType

P = 128
PACK = 4
GROUPS = T2 // (P * PACK)
PASSES = 1 + GROUPS
HALF = 512
CHUNK = 256
TILES = M // P

PASS_ORDER = (2, 1, 3, 0)

WIDEN = {0: ((2, 2),), 1: ((2, 3), (3, 2)), 2: ((3, 3),)}
SCALAR_INTERLEAVE = {2: ((3, 0),), 3: ((3, 2),)}
BEFORE_DIFFERENCE = {1: ((2, 0),)}
AFTER_TURN = {0: ((1, 3),), 1: ((3, 1), (2, 2)), 2: ((2, 3), (3, 3))}
QUANTISE_CHUNK = {2: 2, 4: 3}

PSUM_DIFFERENCE = (1, 2)
WEIGH_LATE = (2, 4)


def tile_pooled_fisher_connectivity_s3_kernel(
    tc,
    seeds_new,
    regions_new,
    seeds_old_bytes,
    seeds_old_scale,
    old_words,
    old_scales,
    precision,
    net_words,
    net_scales,
    out,
):
    nc = tc.nc
    with ExitStack() as ctx:
        keep = ctx.enter_context(tc.tile_pool(name="keep", bufs=1))
        old_pool = ctx.enter_context(tc.tile_pool(name="old", bufs=2 * GROUPS))
        chunk_pool = ctx.enter_context(tc.tile_pool(name="chunks", bufs=M // CHUNK))
        work = ctx.enter_context(tc.tile_pool(name="work", bufs=4))
        psum_r = ctx.enter_context(tc.psum_pool(name="psum_r", bufs=4))
        psum_turn = ctx.enter_context(tc.psum_pool(name="psum_turn", bufs=2))
        psum_out = ctx.enter_context(tc.psum_pool(name="psum_out", bufs=2))
        ctx.enter_context(tc.manual_schedule())

        regions_a = keep.tile([P, PACK, 256], BF16, align_bytes=64)
        regions_b = keep.tile([P, PACK, 256], BF16, align_bytes=64)
        regions_c = keep.tile([P, PACK, HALF], BF16, align_bytes=64)
        region_loads = ((regions_a, 0), (regions_b, 256), (regions_c, HALF))
        new_a = keep.tile([P, PACK, HALF], BF16, align_bytes=64)
        new_b = keep.tile([P, PACK, HALF], BF16, align_bytes=64)
        new_raw = (new_a, new_b)
        old_bytes = {}
        for g in range(GROUPS):
            for half in range(2):
                old_bytes_tile = old_pool.tile([P, PACK, HALF], U8, align_bytes=64)
                old_bytes[g, half] = old_bytes_tile
        old_factor = keep.tile([P, GROUPS, PACK], F32)
        d_words_a = keep.tile([P, GROUPS, 2 * HALF], U8, align_bytes=64)
        d_words_b = keep.tile([P, GROUPS, 2 * HALF], U8, align_bytes=64)
        d_words = (d_words_a, d_words_b)
        d_scales = keep.tile([P, GROUPS, R], U8, align_bytes=64)
        p_words = keep.tile([P, 2, 2 * E], U8, align_bytes=64)
        p_scales = keep.tile([P, 2, E], U8, align_bytes=64)
        weights = keep.tile([P, 2, PACK], BF16)

        regions_grouped = keep.tile([P, R, PACK], BF16, align_bytes=64)
        regions_codes = keep.tile([P, R], U32, align_bytes=64)
        regions_scales = keep.tile([P, R], U8, align_bytes=64)
        wide, grouped, codes, scales = [], [], [], []
        for c in range(M // CHUNK):
            wide_tile = chunk_pool.tile([P, GROUPS, PACK, CHUNK], BF16, align_bytes=64)
            grouped_tile = chunk_pool.tile([P, PASSES, CHUNK, PACK], BF16, align_bytes=64)
            codes_tile = chunk_pool.tile([P, PASSES, CHUNK], U32, align_bytes=64)
            scales_tile = chunk_pool.tile([P, PASSES, CHUNK], U8, align_bytes=64)
            wide.append(wide_tile)
            grouped.append(grouped_tile)
            codes.append(codes_tile)
            scales.append(scales_tile)

        identity = keep.tile([P, P], F32)
        one = keep.tile([P, 1], F32)

        nc.gpsimd.memset(d_scales[:].rearrange("p g n -> p (g n)").bitcast(I32), 0)
        nc.gpsimd.memset(p_scales[:].rearrange("p g n -> p (g n)").bitcast(I32), 0)
        nc.vector.memset(one[:], 1.0)
        make_identity(nc, identity[:])

        def load_regions(j):
            tile, lo = region_loads[j]
            nc.sync.dma_start(
                out=tile[:], in_=regions_new.rearrange("(p t) n -> p t n", t=PACK)[:, :, lo : lo + tile[:].shape[2]]
            )

        def load_new(half):
            nc.sync.dma_start(
                out=new_raw[half][:],
                in_=seeds_new.rearrange("(p t) n -> p t n", t=PACK)[:, :, HALF * half : HALF * half + HALF],
            )

        def load_old(g, half):
            rows = seeds_old_bytes.rearrange("(g p t) n -> g p t n", p=P, t=PACK)[g]
            nc.sync.dma_start(out=old_bytes[g, half][:], in_=rows[:, :, HALF * half : HALF * half + HALF])

        def load_d(half):
            words = old_words.rearrange("g p w -> p g w")
            nc.sync.dma_start(out=d_words[half][:], in_=words[:, :, 2 * HALF * half : 2 * HALF * half + 2 * HALF])

        def load_scale_rows(tile, rows, groups):
            for q in range(4):
                quadrant = tile[32 * q : 32 * q + 4].rearrange("p g n -> p (g n)").bitcast(I32)
                nc.sync.dma_start(
                    out=quadrant.rearrange("p (g n) -> p g n", g=groups),
                    in_=rows[:, 4 * q : 4 * q + 4, :].bitcast(I32).rearrange("g r n -> r g n"),
                )

        nc.scalar.dma_start(
            out=old_factor[:], in_=seeds_old_scale.rearrange("(g p t) o -> p g (t o)", p=P, t=PACK)
        )
        load_old(0, 0)
        load_regions(0)
        load_regions(1)
        load_scale_rows(d_scales, old_scales, GROUPS)
        load_old(1, 0)
        load_old(2, 0)
        load_new(0)
        load_d(0)
        load_d(1)
        load_regions(2)
        for g in range(GROUPS):
            load_old(g, 1)
        load_new(1)
        nc.sync.dma_start(out=p_words[:], in_=net_words.rearrange("g p w -> p g w"))
        load_scale_rows(p_scales, net_scales, 2)
        nc.sync.dma_start(out=weights[:], in_=precision.rearrange("(h p t) -> p h t", p=P, t=PACK))

        nc.scalar.activation(out=one[:], in_=one[:], func=ACT.Ln)

        def widen(c, k):
            cols = slice(CHUNK * (c % 2), CHUNK * (c % 2) + CHUNK)
            for t in range(PACK):
                nc.scalar.activation(
                    out=wide[c][:, k - 1, t, :],
                    in_=old_bytes[k - 1, c // 2][:, t, cols].bitcast(FP8),
                    func=ACT.Copy,
                    scale=old_factor[:, k - 1, t : t + 1],
                )

        def interleave(copy, dst, src):
            copy(out=dst, in_=src.rearrange("p t n -> p n t"))

        def interleave_regions(j):
            tile, lo = region_loads[j]
            interleave(nc.vector.tensor_copy, regions_grouped[:, lo : lo + tile[:].shape[2], :], tile[:])

        def quantise_regions(h):
            cols = slice(HALF * h, HALF * h + HALF)
            nc.vector.quantize_mx(
                out=regions_codes[:, cols].bitcast(FP8X4),
                scales=regions_scales[:, cols],
                in_=regions_grouped[:, cols, :].rearrange("p n t -> p (n t)"),
            )

        def interleave_seeds(c, k, copy=nc.vector.tensor_copy):
            if k == 0:
                src = new_raw[c // 2][:, :, CHUNK * (c % 2) : CHUNK * (c % 2) + CHUNK]
            else:
                src = wide[c][:, k - 1, :, :]
            interleave(copy, grouped[c][:, k, :, :], src)

        def quantise_seeds(c, first, last):
            nc.vector.quantize_mx(
                out=codes[c][:, first:last, :].rearrange("p k n -> p (k n)").bitcast(FP8X4),
                scales=scales[c][:, first:last, :].rearrange("p k n -> p (k n)"),
                in_=grouped[c][:, first:last, :, :].rearrange("p k n t -> p (k n t)"),
            )

        r = {}

        def take_banks(i):
            for h in range(2):
                r_bank = psum_r.tile([P, HALF], F32)
                r[i, h] = r_bank

        def correlate(tiles, h):
            for n, k in enumerate(PASS_ORDER):
                if k == 0:
                    moving = regions_codes[:, HALF * h : HALF * h + HALF].bitcast(FP8X4)
                    moving_scale = regions_scales[:, HALF * h : HALF * h + HALF]
                else:
                    moving = d_words[h][:, k - 1, :].bitcast(FP4X4)
                    moving_scale = d_scales[:, k - 1, HALF * h : HALF * h + HALF]
                for i in tiles:
                    c, j = divmod(i, CHUNK // P)
                    cols = slice(P * j, P * j + P)
                    nc.tensor.matmul_mx(
                        out=r[i, h][:],
                        lhsT=codes[c][:, k, cols].bitcast(FP8X4),
                        lhsT_scale=scales[c][:, k, cols],
                        rhs=moving,
                        rhs_scale=moving_scale,
                        start=(n == 0),
                        stop=(n == PASSES - 1),
                    )

        ln_plus, ln_minus, difference = {}, {}, {}

        def take_logarithms(i, h):
            if h == 0:
                ln_plus_tile = work.tile([P, 2, PACK, P], F32)
                ln_minus_tile = work.tile([P, 2, PACK, P], F32)
                ln_plus[i], ln_minus[i] = ln_plus_tile, ln_minus_tile
            by_t = r[i, h][:].rearrange("s (p t) -> s t p", t=PACK)
            nc.scalar.activation(out=ln_plus[i][:, h], in_=by_t, func=ACT.Ln, bias=1.0, scale=1.0)
            nc.scalar.activation(out=ln_minus[i][:, h], in_=by_t, func=ACT.Ln, bias=1.0, scale=-1.0)

        def form_difference(i, h):
            if h == 0:
                difference_tile = work.tile([P, 2, PACK, P], F32)
                difference[i] = difference_tile
            if i in PSUM_DIFFERENCE:
                nc.vector.tensor_scalar(
                    out=difference[i][:, h], in0=ln_minus[i][:, h], scalar1=-1.0, scalar2=None, op0=ALU.mult
                )
            else:
                nc.vector.tensor_tensor(
                    out=difference[i][:, h], in0=ln_plus[i][:, h], in1=ln_minus[i][:, h], op=ALU.subtract
                )

        turned = {}

        def turn(i, h):
            turned_bank = psum_turn.tile([P, PACK, P], F32)
            turned[i, h] = turned_bank
            parts = (ln_plus[i], difference[i]) if i in PSUM_DIFFERENCE else (difference[i],)
            for t in range(PACK):
                for n, part in enumerate(parts):
                    nc.tensor.matmul(
                        turned_bank[:, t, :],
                        lhsT=part[:, h, t, :],
                        rhs=identity[:],
                        start=(n == 0),
                        stop=(n == len(parts) - 1),
                        is_transpose=True,
                    )

        z_codes, z_scales = {}, {}

        def weigh_and_quantise(i):
            z_grouped = work.tile([P, 2, P, PACK], BF16, align_bytes=64)
            z_codes_tile = work.tile([P, 2, P], U32, align_bytes=64)
            z_scales_tile = work.tile([P, 2, P], U8, align_bytes=64)
            z_codes[i], z_scales[i] = z_codes_tile, z_scales_tile
            for h in range(2):
                nc.vector.tensor_tensor(
                    out=z_grouped[:, h, :, :],
                    in0=turned[i, h][:].rearrange("p t n -> p n t"),
                    in1=weights[:, h, :].unsqueeze(1).to_broadcast([P, P, PACK]),
                    op=ALU.mult,
                )
            for h in range(2):
                nc.vector.quantize_mx(
                    out=z_codes_tile[:, h, :].bitcast(FP8X4),
                    scales=z_scales_tile[:, h, :],
                    in_=z_grouped[:, h, :, :].rearrange("p n t -> p (n t)"),
                )

        out_bank = {}

        def project(i):
            out_bank_tile = psum_out.tile([P, E], F32)
            out_bank[i] = out_bank_tile
            for h in range(2):
                nc.tensor.matmul_mx(
                    out=out_bank_tile[:],
                    lhsT=z_codes[i][:, h, :].bitcast(FP8X4),
                    lhsT_scale=z_scales[i][:, h, :],
                    rhs=p_words[:, h, :].bitcast(FP4X4),
                    rhs_scale=p_scales[:, h, :],
                    start=(h == 0),
                    stop=(h == 1),
                )

        def store(i):
            result = work.tile([P, E], F32)
            nc.scalar.copy(out=result[:], in_=out_bank[i][:])
            nc.sync.dma_start(out=out[P * i : P * i + P, :], in_=result[:])

        def store_in_halves(i):
            result_a = work.tile([P, E // 2], F32)
            result_b = work.tile([P, E // 2], F32)
            nc.scalar.copy(out=result_a[:], in_=out_bank[i][:, : E // 2])
            nc.vector.tensor_copy(out=result_b[:], in_=out_bank[i][:, E // 2 :])
            nc.sync.dma_start(out=out[P * i : P * i + P, : E // 2], in_=result_a[:])
            nc.sync.dma_start(out=out[P * i : P * i + P, E // 2 :], in_=result_b[:])

        for k in range(1, PASSES):
            widen(0, k)
            widen(1, k)
        widen(2, 1)
        widen(3, 1)
        interleave_regions(0)
        interleave_regions(1)
        quantise_regions(0)
        interleave_seeds(0, 1)
        interleave_seeds(0, 2)
        quantise_seeds(0, 1, 2)
        interleave_seeds(0, 0)
        quantise_seeds(0, 2, 3)
        interleave_seeds(1, 0)
        interleave_seeds(0, 3)
        quantise_seeds(0, 0, 1)
        quantise_seeds(0, 3, 4)
        interleave_regions(2)
        quantise_regions(1)
        take_banks(0)
        take_banks(1)
        correlate((0, 1), 0)
        correlate((0, 1), 1)

        for i in range(TILES):
            take_logarithms(i, 0)
            for c, k in WIDEN.get(i, ()):
                widen(c, k)
            take_logarithms(i, 1)
            if i > 1:
                store(i - 2)
            for c, k in SCALAR_INTERLEAVE.get(i, ()):
                interleave_seeds(c, k, nc.scalar.copy)
            if i == 0:
                interleave_seeds(1, 1)
                quantise_seeds(1, 0, 2)
                interleave_seeds(1, 2)
            for c, k in BEFORE_DIFFERENCE.get(i, ()):
                interleave_seeds(c, k)
            form_difference(i, 0)
            form_difference(i, 1)
            if i - 1 in WEIGH_LATE:
                weigh_and_quantise(i - 1)
            turn(i, 0)
            turn(i, 1)
            for c, k in AFTER_TURN.get(i, ()):
                interleave_seeds(c, k)
            if i == 0:
                quantise_seeds(1, 2, 4)
                interleave_seeds(2, 1)
            if i in QUANTISE_CHUNK:
                quantise_seeds(QUANTISE_CHUNK[i], 0, PASSES)
            if i not in WEIGH_LATE:
                weigh_and_quantise(i)
            if i > 0:
                project(i - 1)
            if i + 2 < TILES:
                take_banks(i + 2)
                correlate((i + 2,), 0)
                correlate((i + 2,), 1)
        store(TILES - 2)
        project(TILES - 1)
        store_in_halves(TILES - 1)
